import numpy as np, ml_dtypes
CORES = [0,1,2,3,4,5,6,7,128,129,130,131,132,133,134,135,256,257,258,259,260,261,262,263,384,385,386,387,388,389,390,391]
N = 32
GROUPS = [[0,1,2,3,4,5,6,7],[8,9,10,11,12,13,14,15],[16,17,18,19,20,21,22,23],[24,25,26,27,28,29,30,31]]
def setup_inputs(rng):
    return {"x": rng.standard_normal((N, 128, 256), dtype=np.float32).astype(ml_dtypes.bfloat16)}
def reference(x):
    y = np.empty((N, 128, 2048), x.dtype)
    for g in GROUPS:
        s = np.concatenate([x[r] for r in g], axis=1)
        for r in g:
            y[r] = s
    return {"y": y}

from concourse.bass import DstId, RemoteDMATransfer

SCRATCH = {
    "gather": ("sbuf", [128, 2048], "bfloat16"),
}
SEMAPHORES = ["loaded", "arrived", "stored"]

ENGINES = 16


def rank_program(g, core, T, topo):
    rank = T.rank_of(core)
    if rank is None:
        return
    group = [grp for grp in T.tables["GROUPS"] if rank in grp][0]
    me = group.index(rank)
    w = T.x.shape[1]

    def block(j):
        return T.gather[:, j * w:(j + 1) * w]

    g.sync.dma_start(block(me), T.x[:, :]).then_inc(T.sem.loaded, 16)
    g.wait_ge(T.sem.loaded, 16)

    peers = [T.cores[r] for r in group if r != rank]
    ids = []
    for d in peers:
        rid, pid = topo.addr(d, core)
        ids.append(DstId(rid=rid, pnc=pid))
    g.remote_dma_fused(
        [RemoteDMATransfer(dst_ids=ids, dma_engine_mask=(1 << ENGINES) - 1, remote_sem=T.sem.arrived,
                           srcs=[block(me)], dsts=[block(me) for d in peers])],
        local_sem=T.sem.arrived)

    total = ENGINES * (len(peers) + 1)
    g.sync.wait_ge(T.sem.arrived, total)
    g.sync.dma_start(T.y[:, :], T.gather[:, :]).then_inc(T.sem.stored, 16)
    g.sync.wait_ge(T.sem.stored, 16)
    g.wait_ge(T.sem.arrived, total)
    g.wait_ge(T.sem.stored, 16)
